import numpy as np
import ml_dtypes


def mxq(x, axis, fmt="e4m3"):
    dtype, down = {"e4m3": (ml_dtypes.float8_e4m3fn, 7), "e5m2": (ml_dtypes.float8_e5m2, 14)}[fmt]
    v = np.moveaxis(np.asarray(x, np.float32).astype(ml_dtypes.bfloat16).astype(np.float64), axis, -1)
    blocks = v.reshape(v.shape[:-1] + (-1, 32))
    amax = np.abs(blocks).max(-1, keepdims=True)
    byte = np.maximum(np.where(amax > 0, np.frexp(amax)[1] - 1 + 127, 0) - down, 1)
    scale = np.exp2(byte - 127.0)
    codes = (blocks / scale).astype(np.float32).astype(dtype).astype(np.float64)
    return np.moveaxis((codes * scale).reshape(v.shape), -1, axis)


WIDE = False


def mx_kscale(k):
    if not WIDE:
        return np.ones(k)
    levels = np.array([10, -10, 5, -5, 0])
    if k % 512:
        return np.exp2(np.random.permutation(np.resize(levels, k // 32))).repeat(32)
    a = np.empty((k // 512, 16))
    for p in range(k // 512):
        a[p, :8] = np.random.permutation(np.resize(levels, 8))
        for g in range(8):
            far = levels[np.abs(levels - a[p, g]) >= 10]
            a[p, g + 8] = far[np.random.randint(len(far))]
    return np.exp2(a.ravel()).repeat(32)


def f64(x):
    return np.asarray(x).astype(np.float64)


def striped(idx):
    return np.tile(idx.reshape(-1, 16).T, (8, 1)).astype(np.uint16)


def unstriped(offs):
    return offs[:16].T.reshape(-1).astype(np.int64)


def striped8(idx):
    return np.concatenate([x.reshape(-1, 16).T for x in idx]).astype(np.uint16)


def runs(offs, k):
    lists = np.stack([offs[16 * r : 16 * r + 16].T.reshape(-1) for r in range(8)]).astype(np.int64)
    return lists[np.arange(k) % 512 // 64]


def pack_weight(w):
    k, n = w.shape
    w = f64(np.asarray(w, np.float32).astype(ml_dtypes.bfloat16)).reshape(k // 32, 32, n)
    amax = np.abs(w).max(1)
    byte = np.clip(np.where(amax > 0, np.frexp(amax)[1] - 1 + 127 - 7, 1), 1, 254)
    scaled = (w * np.exp2(127.0 - byte)[:, None, :]).reshape(k, n).astype(np.float32)
    words = np.ascontiguousarray(scaled.reshape(k // 512, 128, 4, n).transpose(0, 1, 3, 2)).astype(ml_dtypes.float8_e4m3fn).view(np.uint8)
    return words, np.ascontiguousarray(byte.astype(np.uint8).reshape(k // 512, 16, n))


def unpack_weight(words, scales):
    g, p, n, _ = words.shape
    vals = np.ascontiguousarray(words).view(ml_dtypes.float8_e4m3fn).astype(np.float64) * np.repeat(np.exp2(scales.astype(np.float64) - 127.0), 8, axis=1)[..., None]
    return vals.transpose(0, 1, 3, 2).reshape(g * 512, n)


def sigmoid(v):
    return 1.0 / (1.0 + np.exp(-np.maximum(v, -700.0)))


K, T, S, N, G, H, W = 512, 1024, 512, 512, 2048, 512, 256


def setup_inputs():
    n = np.random.standard_normal
    s = mx_kscale(K)[:, None]
    u = mx_kscale(S)
    packed_xT = pack_weight(n((K, T)) * s)
    packed_dT = pack_weight(n((K, G)) / s)
    perm = np.random.permutation(S)
    return {
        "x_words": packed_xT[0],
        "x_scales": packed_xT[1],
        "d_words": packed_dT[0],
        "d_scales": packed_dT[1],
        "sl": np.random.uniform(1.0, 2.0, (H, 1)).astype(np.float32),
        "th": (0.5 * n((H, 1))).astype(np.float32),
        "gn": (np.random.uniform(0.5, 1.5, (H, 1)) * u[:, None]).astype(np.float32),
        "w1": (n((H, N)) / np.sqrt(2 * H) / u[:, None]).astype(np.float32),
        "w2": (n((K, N)) / np.sqrt(2 * K) / s).astype(np.float32),
        "sl2": np.random.uniform(1.0, 2.0, (N, 1)).astype(np.float32),
        "th2": (0.5 * n((N, 1))).astype(np.float32),
        "offs": striped(np.random.permutation(T)[:S]),
        "k1": striped8(np.random.randint(0, G, (8, H))),
        "n1": striped(perm[:W]),
        "n2": striped(perm[W:]),
        "two": striped(np.random.permutation(T)[:S]),
        "n3": striped(np.random.permutation(S)),
        "n4": striped(np.random.permutation(S)),
    }


def reference(x_words, x_scales, d_words, d_scales, sl, th, gn, w1, w2, sl2, th2, offs, k1, n1, n2, two, n3, n4):
    d_k1 = unpack_weight(d_words, d_scales)[np.arange(K)[:, None], runs(k1, K)]
    xq = unpack_weight(x_words, x_scales)[:, unstriped(offs)]
    h = 0.0625 * (d_k1.T @ xq)
    pb = h[:, unstriped(n2)]
    sg = sigmoid(f64(sl) * (h[:, unstriped(n1)] - f64(th)))
    rb = pb - sg
    pa = h[:, unstriped(n1)]
    sg2 = sigmoid(f64(sl) * (h[:, unstriped(n2)] - f64(th)))
    ra = pa * sg2
    ds = np.zeros((H, S))
    ds[:, unstriped(n1)] = ra
    dt = ds.copy()
    dt[:, unstriped(n2)] = rb
    z = f64(gn) * dt
    x_two = unpack_weight(x_words, x_scales)[:, unstriped(two)]
    h2 = mxq(f64(w1), 0, "e4m3").T @ mxq(z, 0, "e4m3") + mxq(f64(w2), 0, "e4m3").T @ x_two
    pa2 = h2[:, unstriped(n3)]
    sg3 = sigmoid(f64(sl2) * (h2[:, unstriped(n4)] - f64(th2)))
    return pa2 + sg3 * (h2 - pa2)

@@ -1,0 +1,266 @@
+from contextlib import ExitStack
+
+import concourse.mybir as mybir
+
+K, T, S, N, G, H, W = 512, 1024, 512, 512, 2048, 512, 256
+FLOPS = 2 * (K * H * S + H * N * S + K * N * S)
+
+F32 = mybir.dt.float32
+BF16 = mybir.dt.bfloat16
+I32 = mybir.dt.int32
+U32 = mybir.dt.uint32
+U16 = mybir.dt.uint16
+U8 = mybir.dt.uint8
+FP8X4 = mybir.dt.float8_e4m3fn_x4
+MULT = mybir.AluOpType.mult
+ADD = mybir.AluOpType.add
+SUB = mybir.AluOpType.subtract
+COPY = mybir.ActivationFunctionType.Copy
+SIGMOID = mybir.ActivationFunctionType.Sigmoid
+
+P = 128
+PACK = 4
+TILES = 4
+HALF = S // 2
+SPLIT = 256
+HALVES = (slice(0, HALF), slice(HALF, S))
+LIST_HALVES = (slice(0, HALF // 16), slice(HALF // 16, S // 16))
+
+
+def tile_picked_pqmixeodebl_none_p_kernel(
+    tc, x_words, x_scales, d_words, d_scales, sl, th, gn, w1, w2, sl2, th2, offs, k1, n1, n2, two, n3, n4, out
+):
+    nc = tc.nc
+    with ExitStack() as ctx:
+        keep = ctx.enter_context(tc.tile_pool(name="keep", bufs=1))
+        work = ctx.enter_context(tc.tile_pool(name="work", bufs=1))
+        psum = ctx.enter_context(tc.psum_pool(name="psum", bufs=1))
+
+        def load_list(source, name):
+            offsets = keep.tile(list(source.shape), U16, name=name)
+            nc.sync.dma_start(offsets[:], source)
+            return offsets
+
+        def bank(number, width, name):
+            return psum.tile([P, width], F32, name=name, tag="bank%d" % number)
+
+        def mx(acc, lhs_codes, lhs_scales, rhs_codes, rhs_scales, start, stop):
+            nc.tensor.matmul_mx(
+                out=acc,
+                lhsT=lhs_codes.bitcast(FP8X4),
+                lhsT_scale=lhs_scales,
+                rhs=rhs_codes.bitcast(FP8X4),
+                rhs_scale=rhs_scales,
+                start=start,
+                stop=stop,
+            )
+
+        def load_scale_table(source, width, name):
+            table = work.tile([P, width], U8, name=name)
+            rows = source[0].bitcast(I32)
+            nc.sync.dma_start(table[:].bitcast(I32), rows.unsqueeze(1).to_broadcast([16, 8, width // 4]))
+            return table
+
+        def load_word_table(source, width, name):
+            table = work.tile([P, width], I32, name=name)
+            nc.sync.dma_start(table[:], source[0].rearrange("p c r -> p (c r)").bitcast(I32))
+            return table
+
+        def load_dealt(source, name, tag):
+            column = work.tile([P, TILES], F32, name=name, tag=tag)
+            nc.sync.dma_start(column[:], source.rearrange("(p t) o -> p (t o)", t=TILES))
+            return column
+
+        def place_scale_rows(plane, queue):
+            for a in range(1, 4):
+                queue.dma_start(plane[a:P:32, :].bitcast(I32), plane[8 * a : P : 32, :].bitcast(I32))
+
+        k1_list = load_list(k1, "k1_list")
+        d_scale_table = load_scale_table(d_scales, G, "d_scale_table")
+        offs_list = load_list(offs, "offs_list")
+        x_scale_table = load_scale_table(x_scales, T, "x_scale_table")
+        d_word_table = load_word_table(d_words, G, "d_word_table")
+        n2_list = load_list(n2, "n2_list")
+        n1_list = load_list(n1, "n1_list")
+        slope = load_dealt(sl, "slope", "slope")
+        x_word_table = load_word_table(x_words, T, "x_word_table")
+        threshold = load_dealt(th, "threshold", "threshold")
+        two_list = load_list(two, "two_list")
+        n3_list = load_list(n3, "n3_list")
+        n4_list = load_list(n4, "n4_list")
+
+        def load_plain(source, name, tag):
+            column = work.tile([P, TILES], F32, name=name, tag=tag)
+            with nc.allow_non_contiguous_dma(reason="one value a partition and tile"):
+                nc.sync.dma_start(column[:], source.rearrange("(t p) o -> p (t o)", t=TILES))
+            return column
+
+
+        d_scale_picked = work.tile([P, H], U8, name="d_scale_picked")
+        nc.vector.tensor_copy(d_scale_picked[:], d_scale_table[:].indirect(k1_list[:]))
+        x_scale_gathered = work.tile([P, S], U8, name="x_scale_gathered")
+        nc.vector.tensor_copy(x_scale_gathered[:], x_scale_table[:].indirect(offs_list[:]))
+        planes = work.tile([P, H + S], U8, name="planes", tag="planes", align_bytes=64)
+        d_scale_dealt = planes[:, :H]
+        x_scale_picked = planes[:, H:]
+        nc.vector.tensor_copy(
+            d_scale_dealt.rearrange("p (t m) -> p m t", t=TILES),
+            d_scale_picked[:].rearrange("p (m t) -> p m t", t=TILES),
+        )
+        nc.vector.tensor_copy(x_scale_picked.bitcast(I32), x_scale_gathered[:].bitcast(I32))
+        place_scale_rows(planes, nc.scalar)
+
+        d_word_picked = work.tile([P, H], U32, name="d_word_picked")
+        nc.vector.tensor_copy(d_word_picked[:], d_word_table[:].bitcast(U32).indirect(k1_list[:]))
+        d_word_dealt = work.tile([P, H], U32, name="d_word_dealt", tag="d_word_dealt", align_bytes=64)
+        nc.vector.tensor_copy(
+            d_word_dealt[:].rearrange("p (t m) -> p m t", t=TILES),
+            d_word_picked[:].rearrange("p (m t) -> p m t", t=TILES),
+        )
+
+        x_word_picked = work.tile([P, S], U32, name="x_word_picked", align_bytes=64)
+        h = [work.tile([P, S], F32, name="h%d" % t) for t in range(TILES)]
+        first = slice(0, P)
+        for u in range(2):
+            cols = HALVES[u]
+            nc.vector.tensor_copy(
+                x_word_picked[:, cols], x_word_table[:].bitcast(U32).indirect(offs_list[:, LIST_HALVES[u]])
+            )
+        bias = keep.tile([P, TILES], F32, name="bias")
+        nc.vector.scalar_tensor_tensor(bias[:], slope[:], -1.0, threshold[:], MULT, MULT)
+
+        for u in range(2):
+            cols = HALVES[u]
+            acc = bank(u, HALF, "h0_half%d" % u)
+            mx(acc[:], d_word_dealt[:, first], d_scale_dealt[:, first], x_word_picked[:, cols], x_scale_picked[:, cols], True, True)
+            nc.vector.tensor_scalar(h[0][:, cols], acc[:], 0.0625, None, MULT)
+        for t in range(1, TILES):
+            rows = slice(t * P, (t + 1) * P)
+            acc = bank(t + 1, S, "h%d_sum" % t)
+            mx(acc[:], d_word_dealt[:, rows], d_scale_dealt[:, rows], x_word_picked[:], x_scale_picked, True, True)
+            nc.vector.tensor_scalar(h[t][:], acc[:], 0.0625, None, MULT)
+
+        dt = [work.tile([P, S], F32, name="dt%d" % t) for t in range(TILES)]
+        ra = [work.tile([P, W], F32, name="ra%d" % t) for t in range(TILES)]
+        rb = [work.tile([P, W], F32, name="rb%d" % t) for t in range(TILES)]
+
+        def gate_and_fetch(t, gate_list, fetch_list, name):
+            gate = work.tile([P, W], F32, name="gate_%s%d" % (name, t))
+            fetched = work.tile([P, W], F32, name="fetched_%s%d" % (name, t))
+            nc.scalar.activation(
+                gate[:], h[t][:].indirect(gate_list[:]), SIGMOID, bias=bias[:, t : t + 1], scale=slope[:, t : t + 1]
+            )
+            nc.scalar.activation(fetched[:], h[t][:].indirect(fetch_list[:]), COPY)
+            return gate, fetched
+
+        def make_ra(t):
+            sg2, pa = gate_and_fetch(t, n2_list, n1_list, "a")
+            nc.vector.tensor_tensor(ra[t][:], pa[:], sg2[:], MULT)
+
+        def make_rb(t):
+            sg, pb = gate_and_fetch(t, n1_list, n2_list, "b")
+            nc.vector.tensor_tensor(rb[t][:], pb[:], sg[:], SUB)
+
+        def put_ra(t):
+            nc.scalar.activation(dt[t][:].indirect(n1_list[:]), ra[t][:], COPY)
+
+        def put_rb(t):
+            nc.scalar.activation(dt[t][:].indirect(n2_list[:]), rb[t][:], COPY)
+
+        def round_z(t):
+            for cols in HALVES:
+                nc.vector.tensor_scalar(z[:, cols, t], dt[t][:, cols], gain[:, t : t + 1], None, MULT)
+
+        def quantise_weight(source, name, raw_tag):
+            raw = work.tile([P, PACK, N], F32, name=name + "_raw", tag=raw_tag, align_bytes=64)
+            nc.sync.dma_start(raw[:], source.rearrange("(p j) m -> p j m", j=PACK))
+            codes = work.tile([P, N], U32, name=name + "_codes", align_bytes=64)
+            scales = work.tile([P, N], U8, name=name + "_scales", align_bytes=64)
+            grouped = work.tile([P, N, PACK], BF16, name=name + "_grouped", tag=name + "_grouped", align_bytes=64)
+            for cols in HALVES:
+                nc.vector.tensor_copy(grouped[:, cols, :], raw[:, :, cols].rearrange("p j m -> p m j"))
+            for cols in HALVES:
+                nc.vector.quantize_mx(
+                    out=codes[:, cols].bitcast(FP8X4), scales=scales[:, cols], in_=grouped[:, cols, :].rearrange("p m j -> p (m j)")
+                )
+            return codes, scales
+
+        for t in range(TILES):
+            make_ra(t)
+            make_rb(t)
+        gain = load_dealt(gn, "gain", "gate_a0")
+        slope2 = load_plain(sl2, "slope2", "fetched_a0")
+        threshold2 = load_plain(th2, "threshold2", "gate_b0")
+
+        two_words = work.tile([P, S], U32, name="two_words", align_bytes=64)
+        two_scales_gathered = work.tile([P, S], U8, name="two_scales_gathered")
+        two_scales = work.tile([P, S], U8, name="two_scales", align_bytes=64)
+        for u in range(2):
+            nc.vector.tensor_copy(
+                two_words[:, HALVES[u]], x_word_table[:].bitcast(U32).indirect(two_list[:, LIST_HALVES[u]])
+            )
+            nc.vector.tensor_copy(two_scales_gathered[:, HALVES[u]], x_scale_table[:].indirect(two_list[:, LIST_HALVES[u]]))
+        nc.vector.tensor_copy(two_scales[:].bitcast(I32), two_scales_gathered[:].bitcast(I32))
+        place_scale_rows(two_scales, nc.sync)
+        w2_codes, w2_scales = quantise_weight(w2, "w2", "planes")
+        w1_codes, w1_scales = quantise_weight(w1, "w1", "d_word_dealt")
+        z = work.tile([P, S, PACK], BF16, name="z", tag="w1_grouped", align_bytes=64)
+        bias2 = keep.tile([P, TILES], F32, name="bias2")
+        nc.vector.scalar_tensor_tensor(bias2[:], slope2[:], -1.0, threshold2[:], MULT, MULT)
+
+        first_sums = [bank(5 + u, HALF, "h2_0_half%d" % u) for u in range(2)]
+        sums = [bank((6 + t) % 8, S, "h2_%d_sum" % t) for t in range(1, TILES)]
+        for u in range(2):
+            cols = HALVES[u]
+            mx(first_sums[u][:], w2_codes[:, first], w2_scales[:, first], two_words[:, cols], two_scales[:, cols], True, False)
+        for t in range(1, TILES):
+            rows = slice(t * P, (t + 1) * P)
+            mx(sums[t - 1][:], w2_codes[:, rows], w2_scales[:, rows], two_words[:], two_scales[:], True, False)
+
+        put_ra(0)
+        for t in range(TILES):
+            if t + 1 < TILES:
+                put_ra(t + 1)
+            put_rb(t)
+            round_z(t)
+
+        z_codes = work.tile([P, S], U32, name="z_codes", align_bytes=64)
+        z_scales = work.tile([P, S], U8, name="z_scales", align_bytes=64)
+        for cols in HALVES:
+            nc.vector.quantize_mx(
+                out=z_codes[:, cols].bitcast(FP8X4), scales=z_scales[:, cols], in_=z[:, cols, :].rearrange("p j t -> p (j t)")
+            )
+
+        h2 = [work.tile([P, S], F32, name="h2_%d" % t) for t in range(TILES)]
+        for u in range(2):
+            cols = HALVES[u]
+            mx(first_sums[u][:], w1_codes[:, first], w1_scales[:, first], z_codes[:, cols], z_scales[:, cols], False, True)
+        for t in range(1, TILES):
+            rows = slice(t * P, (t + 1) * P)
+            mx(sums[t - 1][:], w1_codes[:, rows], w1_scales[:, rows], z_codes[:], z_scales[:], False, True)
+        nc.scalar.activation(h2[0][:, HALVES[0]], first_sums[0][:], COPY)
+        nc.vector.tensor_copy(h2[0][:, HALVES[1]], first_sums[1][:])
+
+        for t in range(TILES):
+            pa2 = work.tile([P, S], F32, name="pa2_%d" % t)
+            sg3 = [work.tile([P, HALF], F32, name="sg3_%d_%d" % (t, u)) for u in range(2)]
+            diff = [work.tile([P, HALF], F32, name="diff_%d_%d" % (t, u)) for u in range(2)]
+            gated = [work.tile([P, HALF], F32, name="gated_%d_%d" % (t, u)) for u in range(2)]
+            result = [work.tile([P, HALF], F32, name="result_%d_%d" % (t, u)) for u in range(2)]
+            nc.vector.tensor_copy(pa2[:, :SPLIT], h2[t][:].indirect(n3_list[:, : SPLIT // 16]))
+            nc.scalar.activation(
+                sg3[0][:], h2[t][:].indirect(n4_list[:, LIST_HALVES[0]]), SIGMOID, bias=bias2[:, t : t + 1], scale=slope2[:, t : t + 1]
+            )
+            nc.scalar.activation(pa2[:, SPLIT:], h2[t][:].indirect(n3_list[:, SPLIT // 16 :]), COPY)
+            nc.scalar.activation(
+                sg3[1][:], h2[t][:].indirect(n4_list[:, LIST_HALVES[1]]), SIGMOID, bias=bias2[:, t : t + 1], scale=slope2[:, t : t + 1]
+            )
+            if t + 1 < TILES:
+                nc.scalar.activation(h2[t + 1][:], sums[t][:], COPY)
+            for u in range(2):
+                nc.vector.tensor_tensor(diff[u][:], h2[t][:, HALVES[u]], pa2[:, HALVES[u]], SUB)
+            for u in range(2):
+                nc.vector.tensor_tensor(gated[u][:], diff[u][:], sg3[u][:], MULT)
+            for u in range(2):
+                nc.vector.tensor_tensor(result[u][:], gated[u][:], pa2[:, HALVES[u]], ADD)
+                nc.sync.dma_start(out[t * P : (t + 1) * P, HALVES[u]], result[u][:])

@@ -24,7 +24,13 @@ TILES = 4
 HALF = S // 2
 SPLIT = 256
 HALVES = (slice(0, HALF), slice(HALF, S))
+QUARTERS = [slice(u * P, (u + 1) * P) for u in range(4)]
+TAPERED = (HALVES[0], QUARTERS[2], QUARTERS[3])
 LIST_HALVES = (slice(0, HALF // 16), slice(HALF // 16, S // 16))
+
+
+def entries(cols):
+    return slice(cols.start // 16, cols.stop // 16)
 
 
 def tile_picked_pqmixeodebl_none_p_kernel(
@@ -71,14 +77,14 @@ def tile_picked_pqmixeodebl_none_p_kernel(
             nc.sync.dma_start(column[:], source.rearrange("(p t) o -> p (t o)", t=TILES))
             return column
 
-        def place_scale_rows(plane, queue):
-            for a in range(1, 4):
+        def place_scale_rows(plane, queues):
+            for a, queue in zip(range(1, 4), queues):
                 queue.dma_start(plane[a:P:32, :].bitcast(I32), plane[8 * a : P : 32, :].bitcast(I32))
 
-        k1_list = load_list(k1, "k1_list")
-        d_scale_table = load_scale_table(d_scales, G, "d_scale_table")
         offs_list = load_list(offs, "offs_list")
         x_scale_table = load_scale_table(x_scales, T, "x_scale_table")
+        k1_list = load_list(k1, "k1_list")
+        d_scale_table = load_scale_table(d_scales, G, "d_scale_table")
         d_word_table = load_word_table(d_words, G, "d_word_table")
         n2_list = load_list(n2, "n2_list")
         n1_list = load_list(n1, "n1_list")
@@ -96,42 +102,43 @@ def tile_picked_pqmixeodebl_none_p_kernel(
             return column
 
 
-        d_scale_picked = work.tile([P, H], U8, name="d_scale_picked")
-        nc.vector.tensor_copy(d_scale_picked[:], d_scale_table[:].indirect(k1_list[:]))
         x_scale_gathered = work.tile([P, S], U8, name="x_scale_gathered")
         nc.vector.tensor_copy(x_scale_gathered[:], x_scale_table[:].indirect(offs_list[:]))
+        d_scale_picked = work.tile([P, H], U8, name="d_scale_picked")
+        nc.vector.tensor_copy(d_scale_picked[:], d_scale_table[:].indirect(k1_list[:]))
         planes = work.tile([P, H + S], U8, name="planes", tag="planes", align_bytes=64)
         d_scale_dealt = planes[:, :H]
         x_scale_picked = planes[:, H:]
-        nc.vector.tensor_copy(
-            d_scale_dealt.rearrange("p (t m) -> p m t", t=TILES),
-            d_scale_picked[:].rearrange("p (m t) -> p m t", t=TILES),
-        )
         nc.vector.tensor_copy(x_scale_picked.bitcast(I32), x_scale_gathered[:].bitcast(I32))
-        place_scale_rows(planes, nc.scalar)
+        nc.vector.tensor_copy(
+            d_scale_dealt.rearrange("p (t m) -> p t m", t=TILES),
+            d_scale_picked[:].rearrange("p (m t) -> p t m", t=TILES),
+        )
+        place_scale_rows(planes, (nc.scalar, nc.scalar, nc.scalar))
 
         d_word_picked = work.tile([P, H], U32, name="d_word_picked")
         nc.vector.tensor_copy(d_word_picked[:], d_word_table[:].bitcast(U32).indirect(k1_list[:]))
+        x_word_picked = work.tile([P, S], U32, name="x_word_picked", align_bytes=64)
+
+        def pick_x_words(cols):
+            nc.vector.tensor_copy(x_word_picked[:, cols], x_word_table[:].bitcast(U32).indirect(offs_list[:, entries(cols)]))
+
+        pick_x_words(TAPERED[0])
         d_word_dealt = work.tile([P, H], U32, name="d_word_dealt", tag="d_word_dealt", align_bytes=64)
         nc.vector.tensor_copy(
             d_word_dealt[:].rearrange("p (t m) -> p m t", t=TILES),
             d_word_picked[:].rearrange("p (m t) -> p m t", t=TILES),
         )
+        pick_x_words(TAPERED[1])
+        pick_x_words(TAPERED[2])
 
-        x_word_picked = work.tile([P, S], U32, name="x_word_picked", align_bytes=64)
-        h = [work.tile([P, S], F32, name="h%d" % t) for t in range(TILES)]
-        first = slice(0, P)
-        for u in range(2):
-            cols = HALVES[u]
-            nc.vector.tensor_copy(
-                x_word_picked[:, cols], x_word_table[:].bitcast(U32).indirect(offs_list[:, LIST_HALVES[u]])
-            )
         bias = keep.tile([P, TILES], F32, name="bias")
         nc.vector.scalar_tensor_tensor(bias[:], slope[:], -1.0, threshold[:], MULT, MULT)
 
-        for u in range(2):
-            cols = HALVES[u]
-            acc = bank(u, HALF, "h0_half%d" % u)
+        h = [work.tile([P, S], F32, name="h%d" % t) for t in range(TILES)]
+        first = slice(0, P)
+        for u, cols in enumerate(TAPERED):
+            acc = bank((0, 1, 5)[u], cols.stop - cols.start, "h0_piece%d" % u)
             mx(acc[:], d_word_dealt[:, first], d_scale_dealt[:, first], x_word_picked[:, cols], x_scale_picked[:, cols], True, True)
             nc.vector.tensor_scalar(h[0][:, cols], acc[:], 0.0625, None, MULT)
         for t in range(1, TILES):
@@ -167,8 +174,8 @@ def tile_picked_pqmixeodebl_none_p_kernel(
         def put_rb(t):
             nc.scalar.activation(dt[t][:].indirect(n2_list[:]), rb[t][:], COPY)
 
-        def round_z(t):
-            for cols in HALVES:
+        def round_z(t, pieces):
+            for cols in pieces:
                 nc.vector.tensor_scalar(z[:, cols, t], dt[t][:, cols], gain[:, t : t + 1], None, MULT)
 
         def quantise_weight(source, name, raw_tag):
@@ -201,17 +208,17 @@ def tile_picked_pqmixeodebl_none_p_kernel(
             )
             nc.vector.tensor_copy(two_scales_gathered[:, HALVES[u]], x_scale_table[:].indirect(two_list[:, LIST_HALVES[u]]))
         nc.vector.tensor_copy(two_scales[:].bitcast(I32), two_scales_gathered[:].bitcast(I32))
-        place_scale_rows(two_scales, nc.sync)
+        place_scale_rows(two_scales, (nc.sync, nc.sync, nc.sync))
         w2_codes, w2_scales = quantise_weight(w2, "w2", "planes")
         w1_codes, w1_scales = quantise_weight(w1, "w1", "d_word_dealt")
         z = work.tile([P, S, PACK], BF16, name="z", tag="w1_grouped", align_bytes=64)
         bias2 = keep.tile([P, TILES], F32, name="bias2")
         nc.vector.scalar_tensor_tensor(bias2[:], slope2[:], -1.0, threshold2[:], MULT, MULT)
 
-        first_sums = [bank(5 + u, HALF, "h2_0_half%d" % u) for u in range(2)]
-        sums = [bank((6 + t) % 8, S, "h2_%d_sum" % t) for t in range(1, TILES)]
-        for u in range(2):
-            cols = HALVES[u]
+        first_sums = [bank((5 + u) % 8, P, "h2_0_quarter%d" % u) for u in range(4)]
+        sums = [bank(t, S, "h2_%d_sum" % t) for t in range(1, TILES)]
+        for u in range(4):
+            cols = QUARTERS[u]
             mx(first_sums[u][:], w2_codes[:, first], w2_scales[:, first], two_words[:, cols], two_scales[:, cols], True, False)
         for t in range(1, TILES):
             rows = slice(t * P, (t + 1) * P)
@@ -222,45 +229,68 @@ def tile_picked_pqmixeodebl_none_p_kernel(
             if t + 1 < TILES:
                 put_ra(t + 1)
             put_rb(t)
-            round_z(t)
+            if t + 1 < TILES:
+                round_z(t, HALVES)
 
         z_codes = work.tile([P, S], U32, name="z_codes", align_bytes=64)
         z_scales = work.tile([P, S], U8, name="z_scales", align_bytes=64)
-        for cols in HALVES:
+        h2 = [work.tile([P, S], F32, name="h2_%d" % t) for t in range(TILES)]
+
+        def finish_quarter(u):
+            cols = QUARTERS[u]
             nc.vector.quantize_mx(
                 out=z_codes[:, cols].bitcast(FP8X4), scales=z_scales[:, cols], in_=z[:, cols, :].rearrange("p j t -> p (j t)")
             )
-
-        h2 = [work.tile([P, S], F32, name="h2_%d" % t) for t in range(TILES)]
-        for u in range(2):
-            cols = HALVES[u]
             mx(first_sums[u][:], w1_codes[:, first], w1_scales[:, first], z_codes[:, cols], z_scales[:, cols], False, True)
+            nc.scalar.activation(h2[0][:, cols], first_sums[u][:], COPY)
+
+        for u in range(4):
+            round_z(TILES - 1, [QUARTERS[u]])
+            if u > 0:
+                finish_quarter(u - 1)
+        finish_quarter(3)
         for t in range(1, TILES):
             rows = slice(t * P, (t + 1) * P)
             mx(sums[t - 1][:], w1_codes[:, rows], w1_scales[:, rows], z_codes[:], z_scales[:], False, True)
-        nc.scalar.activation(h2[0][:, HALVES[0]], first_sums[0][:], COPY)
-        nc.vector.tensor_copy(h2[0][:, HALVES[1]], first_sums[1][:])
 
+        pa2, sg3, diff, gated, result = [
+            [work.tile([P, S], F32, name="%s_%d" % (name, t)) for t in range(TILES)]
+            for name in ("pa2", "sg3", "diff", "gated", "result")
+        ]
+
+        def fetch_gate(t, cols):
+            nc.scalar.activation(
+                sg3[t][:, cols], h2[t][:].indirect(n4_list[:, entries(cols)]), SIGMOID, bias=bias2[:, t : t + 1], scale=slope2[:, t : t + 1]
+            )
+
+        def subtract(t, cols):
+            nc.vector.tensor_tensor(diff[t][:, cols], h2[t][:, cols], pa2[t][:, cols], SUB)
+
+        def gate(t, cols):
+            nc.vector.tensor_tensor(gated[t][:, cols], diff[t][:, cols], sg3[t][:, cols], MULT)
+
+        def finish(t, cols):
+            nc.vector.tensor_tensor(result[t][:, cols], gated[t][:, cols], pa2[t][:, cols], ADD)
+            nc.sync.dma_start(out[t * P : (t + 1) * P, cols], result[t][:, cols])
+
+        low, high = HALVES
         for t in range(TILES):
-            pa2 = work.tile([P, S], F32, name="pa2_%d" % t)
-            sg3 = [work.tile([P, HALF], F32, name="sg3_%d_%d" % (t, u)) for u in range(2)]
-            diff = [work.tile([P, HALF], F32, name="diff_%d_%d" % (t, u)) for u in range(2)]
-            gated = [work.tile([P, HALF], F32, name="gated_%d_%d" % (t, u)) for u in range(2)]
-            result = [work.tile([P, HALF], F32, name="result_%d_%d" % (t, u)) for u in range(2)]
-            nc.vector.tensor_copy(pa2[:, :SPLIT], h2[t][:].indirect(n3_list[:, : SPLIT // 16]))
-            nc.scalar.activation(
-                sg3[0][:], h2[t][:].indirect(n4_list[:, LIST_HALVES[0]]), SIGMOID, bias=bias2[:, t : t + 1], scale=slope2[:, t : t + 1]
-            )
-            nc.scalar.activation(pa2[:, SPLIT:], h2[t][:].indirect(n3_list[:, SPLIT // 16 :]), COPY)
-            nc.scalar.activation(
-                sg3[1][:], h2[t][:].indirect(n4_list[:, LIST_HALVES[1]]), SIGMOID, bias=bias2[:, t : t + 1], scale=slope2[:, t : t + 1]
-            )
-            if t + 1 < TILES:
-                nc.scalar.activation(h2[t + 1][:], sums[t][:], COPY)
-            for u in range(2):
-                nc.vector.tensor_tensor(diff[u][:], h2[t][:, HALVES[u]], pa2[:, HALVES[u]], SUB)
-            for u in range(2):
-                nc.vector.tensor_tensor(gated[u][:], diff[u][:], sg3[u][:], MULT)
-            for u in range(2):
-                nc.vector.tensor_tensor(result[u][:], gated[u][:], pa2[:, HALVES[u]], ADD)
-                nc.sync.dma_start(out[t * P : (t + 1) * P, HALVES[u]], result[u][:])
+            if t > 0:
+                nc.scalar.activation(h2[t][:], sums[t - 1][:], COPY)
+            nc.vector.tensor_copy(pa2[t][:, :SPLIT], h2[t][:].indirect(n3_list[:, : SPLIT // 16]))
+            if t > 0:
+                fetch_gate(t - 1, high)
+                gate(t - 1, high)
+            fetch_gate(t, low)
+            subtract(t, low)
+            if t > 0:
+                finish(t - 1, high)
+            nc.scalar.activation(pa2[t][:, SPLIT:], h2[t][:].indirect(n3_list[:, SPLIT // 16 :]), COPY)
+            gate(t, low)
+            subtract(t, high)
+            finish(t, low)
+        for cols in QUARTERS[2:]:
+            fetch_gate(TILES - 1, cols)
+            gate(TILES - 1, cols)
+        for cols in QUARTERS[2:]:
+            finish(TILES - 1, cols)

from contextlib import ExitStack

import concourse.mybir as mybir

K, T, S, N, G, H, W = 512, 1024, 512, 512, 2048, 512, 256
FLOPS = 2 * (K * H * S + H * N * S + K * N * S)

F32 = mybir.dt.float32
BF16 = mybir.dt.bfloat16
I32 = mybir.dt.int32
U32 = mybir.dt.uint32
U16 = mybir.dt.uint16
U8 = mybir.dt.uint8
FP8X4 = mybir.dt.float8_e4m3fn_x4
MULT = mybir.AluOpType.mult
ADD = mybir.AluOpType.add
SUB = mybir.AluOpType.subtract
COPY = mybir.ActivationFunctionType.Copy
SIGMOID = mybir.ActivationFunctionType.Sigmoid

P = 128
PACK = 4
TILES = 4
HALF = S // 2
SPLIT = 256
HALVES = (slice(0, HALF), slice(HALF, S))
QUARTERS = [slice(u * P, (u + 1) * P) for u in range(4)]
TAPERED = (HALVES[0], QUARTERS[2], QUARTERS[3])
LIST_HALVES = (slice(0, HALF // 16), slice(HALF // 16, S // 16))


def entries(cols):
    return slice(cols.start // 16, cols.stop // 16)


def tile_picked_pqmixeodebl_none_p_kernel(
    tc, x_words, x_scales, d_words, d_scales, sl, th, gn, w1, w2, sl2, th2, offs, k1, n1, n2, two, n3, n4, out
):
    nc = tc.nc
    with ExitStack() as ctx:
        keep = ctx.enter_context(tc.tile_pool(name="keep", bufs=1))
        work = ctx.enter_context(tc.tile_pool(name="work", bufs=1))
        psum = ctx.enter_context(tc.psum_pool(name="psum", bufs=1))

        def load_list(source, name):
            offsets = keep.tile(list(source.shape), U16, name=name)
            nc.sync.dma_start(offsets[:], source)
            return offsets

        def bank(number, width, name):
            return psum.tile([P, width], F32, name=name, tag="bank%d" % number)

        def mx(acc, lhs_codes, lhs_scales, rhs_codes, rhs_scales, start, stop):
            nc.tensor.matmul_mx(
                out=acc,
                lhsT=lhs_codes.bitcast(FP8X4),
                lhsT_scale=lhs_scales,
                rhs=rhs_codes.bitcast(FP8X4),
                rhs_scale=rhs_scales,
                start=start,
                stop=stop,
            )

        def load_scale_table(source, width, name):
            table = work.tile([P, width], U8, name=name)
            rows = source[0].bitcast(I32)
            nc.sync.dma_start(table[:].bitcast(I32), rows.unsqueeze(1).to_broadcast([16, 8, width // 4]))
            return table

        def load_word_table(source, width, name):
            table = work.tile([P, width], I32, name=name)
            nc.sync.dma_start(table[:], source[0].rearrange("p c r -> p (c r)").bitcast(I32))
            return table

        def load_dealt(source, name, tag):
            column = work.tile([P, TILES], F32, name=name, tag=tag)
            nc.sync.dma_start(column[:], source.rearrange("(p t) o -> p (t o)", t=TILES))
            return column

        def place_scale_rows(plane, queues):
            for a, queue in zip(range(1, 4), queues):
                queue.dma_start(plane[a:P:32, :].bitcast(I32), plane[8 * a : P : 32, :].bitcast(I32))

        offs_list = load_list(offs, "offs_list")
        x_scale_table = load_scale_table(x_scales, T, "x_scale_table")
        k1_list = load_list(k1, "k1_list")
        d_scale_table = load_scale_table(d_scales, G, "d_scale_table")
        d_word_table = load_word_table(d_words, G, "d_word_table")
        n2_list = load_list(n2, "n2_list")
        n1_list = load_list(n1, "n1_list")
        slope = load_dealt(sl, "slope", "slope")
        x_word_table = load_word_table(x_words, T, "x_word_table")
        threshold = load_dealt(th, "threshold", "threshold")
        two_list = load_list(two, "two_list")
        n3_list = load_list(n3, "n3_list")
        n4_list = load_list(n4, "n4_list")

        def load_plain(source, name, tag):
            column = work.tile([P, TILES], F32, name=name, tag=tag)
            with nc.allow_non_contiguous_dma(reason="one value a partition and tile"):
                nc.sync.dma_start(column[:], source.rearrange("(t p) o -> p (t o)", t=TILES))
            return column


        x_scale_gathered = work.tile([P, S], U8, name="x_scale_gathered")
        nc.vector.tensor_copy(x_scale_gathered[:], x_scale_table[:].indirect(offs_list[:]))
        d_scale_picked = work.tile([P, H], U8, name="d_scale_picked")
        nc.vector.tensor_copy(d_scale_picked[:], d_scale_table[:].indirect(k1_list[:]))
        planes = work.tile([P, H + S], U8, name="planes", tag="planes", align_bytes=64)
        d_scale_dealt = planes[:, :H]
        x_scale_picked = planes[:, H:]
        nc.vector.tensor_copy(x_scale_picked.bitcast(I32), x_scale_gathered[:].bitcast(I32))
        nc.vector.tensor_copy(
            d_scale_dealt.rearrange("p (t m) -> p t m", t=TILES),
            d_scale_picked[:].rearrange("p (m t) -> p t m", t=TILES),
        )
        place_scale_rows(planes, (nc.scalar, nc.scalar, nc.scalar))

        d_word_picked = work.tile([P, H], U32, name="d_word_picked")
        nc.vector.tensor_copy(d_word_picked[:], d_word_table[:].bitcast(U32).indirect(k1_list[:]))
        x_word_picked = work.tile([P, S], U32, name="x_word_picked", align_bytes=64)

        def pick_x_words(cols):
            nc.vector.tensor_copy(x_word_picked[:, cols], x_word_table[:].bitcast(U32).indirect(offs_list[:, entries(cols)]))

        pick_x_words(TAPERED[0])
        d_word_dealt = work.tile([P, H], U32, name="d_word_dealt", tag="d_word_dealt", align_bytes=64)
        nc.vector.tensor_copy(
            d_word_dealt[:].rearrange("p (t m) -> p m t", t=TILES),
            d_word_picked[:].rearrange("p (m t) -> p m t", t=TILES),
        )
        pick_x_words(TAPERED[1])
        pick_x_words(TAPERED[2])

        bias = keep.tile([P, TILES], F32, name="bias")
        nc.vector.scalar_tensor_tensor(bias[:], slope[:], -1.0, threshold[:], MULT, MULT)

        h = [work.tile([P, S], F32, name="h%d" % t) for t in range(TILES)]
        first = slice(0, P)
        for u, cols in enumerate(TAPERED):
            acc = bank((0, 1, 5)[u], cols.stop - cols.start, "h0_piece%d" % u)
            mx(acc[:], d_word_dealt[:, first], d_scale_dealt[:, first], x_word_picked[:, cols], x_scale_picked[:, cols], True, True)
            nc.vector.tensor_scalar(h[0][:, cols], acc[:], 0.0625, None, MULT)
        for t in range(1, TILES):
            rows = slice(t * P, (t + 1) * P)
            acc = bank(t + 1, S, "h%d_sum" % t)
            mx(acc[:], d_word_dealt[:, rows], d_scale_dealt[:, rows], x_word_picked[:], x_scale_picked, True, True)
            nc.vector.tensor_scalar(h[t][:], acc[:], 0.0625, None, MULT)

        dt = [work.tile([P, S], F32, name="dt%d" % t) for t in range(TILES)]
        ra = [work.tile([P, W], F32, name="ra%d" % t) for t in range(TILES)]
        rb = [work.tile([P, W], F32, name="rb%d" % t) for t in range(TILES)]

        def gate_and_fetch(t, gate_list, fetch_list, name):
            gate = work.tile([P, W], F32, name="gate_%s%d" % (name, t))
            fetched = work.tile([P, W], F32, name="fetched_%s%d" % (name, t))
            nc.scalar.activation(
                gate[:], h[t][:].indirect(gate_list[:]), SIGMOID, bias=bias[:, t : t + 1], scale=slope[:, t : t + 1]
            )
            nc.scalar.activation(fetched[:], h[t][:].indirect(fetch_list[:]), COPY)
            return gate, fetched

        def make_ra(t):
            sg2, pa = gate_and_fetch(t, n2_list, n1_list, "a")
            nc.vector.tensor_tensor(ra[t][:], pa[:], sg2[:], MULT)

        def make_rb(t):
            sg, pb = gate_and_fetch(t, n1_list, n2_list, "b")
            nc.vector.tensor_tensor(rb[t][:], pb[:], sg[:], SUB)

        def put_ra(t):
            nc.scalar.activation(dt[t][:].indirect(n1_list[:]), ra[t][:], COPY)

        def put_rb(t):
            nc.scalar.activation(dt[t][:].indirect(n2_list[:]), rb[t][:], COPY)

        def round_z(t, pieces):
            for cols in pieces:
                nc.vector.tensor_scalar(z[:, cols, t], dt[t][:, cols], gain[:, t : t + 1], None, MULT)

        def quantise_weight(source, name, raw_tag):
            raw = work.tile([P, PACK, N], F32, name=name + "_raw", tag=raw_tag, align_bytes=64)
            nc.sync.dma_start(raw[:], source.rearrange("(p j) m -> p j m", j=PACK))
            codes = work.tile([P, N], U32, name=name + "_codes", align_bytes=64)
            scales = work.tile([P, N], U8, name=name + "_scales", align_bytes=64)
            grouped = work.tile([P, N, PACK], BF16, name=name + "_grouped", tag=name + "_grouped", align_bytes=64)
            for cols in HALVES:
                nc.vector.tensor_copy(grouped[:, cols, :], raw[:, :, cols].rearrange("p j m -> p m j"))
            for cols in HALVES:
                nc.vector.quantize_mx(
                    out=codes[:, cols].bitcast(FP8X4), scales=scales[:, cols], in_=grouped[:, cols, :].rearrange("p m j -> p (m j)")
                )
            return codes, scales

        for t in range(TILES):
            make_ra(t)
            make_rb(t)
        gain = load_dealt(gn, "gain", "gate_a0")
        slope2 = load_plain(sl2, "slope2", "fetched_a0")
        threshold2 = load_plain(th2, "threshold2", "gate_b0")

        two_words = work.tile([P, S], U32, name="two_words", align_bytes=64)
        two_scales_gathered = work.tile([P, S], U8, name="two_scales_gathered")
        two_scales = work.tile([P, S], U8, name="two_scales", align_bytes=64)
        for u in range(2):
            nc.vector.tensor_copy(
                two_words[:, HALVES[u]], x_word_table[:].bitcast(U32).indirect(two_list[:, LIST_HALVES[u]])
            )
            nc.vector.tensor_copy(two_scales_gathered[:, HALVES[u]], x_scale_table[:].indirect(two_list[:, LIST_HALVES[u]]))
        nc.vector.tensor_copy(two_scales[:].bitcast(I32), two_scales_gathered[:].bitcast(I32))
        place_scale_rows(two_scales, (nc.sync, nc.sync, nc.sync))
        w2_codes, w2_scales = quantise_weight(w2, "w2", "planes")
        w1_codes, w1_scales = quantise_weight(w1, "w1", "d_word_dealt")
        z = work.tile([P, S, PACK], BF16, name="z", tag="w1_grouped", align_bytes=64)
        bias2 = keep.tile([P, TILES], F32, name="bias2")
        nc.vector.scalar_tensor_tensor(bias2[:], slope2[:], -1.0, threshold2[:], MULT, MULT)

        first_sums = [bank((5 + u) % 8, P, "h2_0_quarter%d" % u) for u in range(4)]
        sums = [bank(t, S, "h2_%d_sum" % t) for t in range(1, TILES)]
        for u in range(4):
            cols = QUARTERS[u]
            mx(first_sums[u][:], w2_codes[:, first], w2_scales[:, first], two_words[:, cols], two_scales[:, cols], True, False)
        for t in range(1, TILES):
            rows = slice(t * P, (t + 1) * P)
            mx(sums[t - 1][:], w2_codes[:, rows], w2_scales[:, rows], two_words[:], two_scales[:], True, False)

        put_ra(0)
        for t in range(TILES):
            if t + 1 < TILES:
                put_ra(t + 1)
            put_rb(t)
            if t + 1 < TILES:
                round_z(t, HALVES)

        z_codes = work.tile([P, S], U32, name="z_codes", align_bytes=64)
        z_scales = work.tile([P, S], U8, name="z_scales", align_bytes=64)
        h2 = [work.tile([P, S], F32, name="h2_%d" % t) for t in range(TILES)]

        def finish_quarter(u):
            cols = QUARTERS[u]
            nc.vector.quantize_mx(
                out=z_codes[:, cols].bitcast(FP8X4), scales=z_scales[:, cols], in_=z[:, cols, :].rearrange("p j t -> p (j t)")
            )
            mx(first_sums[u][:], w1_codes[:, first], w1_scales[:, first], z_codes[:, cols], z_scales[:, cols], False, True)
            nc.scalar.activation(h2[0][:, cols], first_sums[u][:], COPY)

        for u in range(4):
            round_z(TILES - 1, [QUARTERS[u]])
            if u > 0:
                finish_quarter(u - 1)
        finish_quarter(3)
        for t in range(1, TILES):
            rows = slice(t * P, (t + 1) * P)
            mx(sums[t - 1][:], w1_codes[:, rows], w1_scales[:, rows], z_codes[:], z_scales[:], False, True)

        pa2, sg3, diff, gated, result = [
            [work.tile([P, S], F32, name="%s_%d" % (name, t)) for t in range(TILES)]
            for name in ("pa2", "sg3", "diff", "gated", "result")
        ]

        def fetch_gate(t, cols):
            nc.scalar.activation(
                sg3[t][:, cols], h2[t][:].indirect(n4_list[:, entries(cols)]), SIGMOID, bias=bias2[:, t : t + 1], scale=slope2[:, t : t + 1]
            )

        def subtract(t, cols):
            nc.vector.tensor_tensor(diff[t][:, cols], h2[t][:, cols], pa2[t][:, cols], SUB)

        def gate(t, cols):
            nc.vector.tensor_tensor(gated[t][:, cols], diff[t][:, cols], sg3[t][:, cols], MULT)

        def finish(t, cols):
            nc.vector.tensor_tensor(result[t][:, cols], gated[t][:, cols], pa2[t][:, cols], ADD)
            nc.sync.dma_start(out[t * P : (t + 1) * P, cols], result[t][:, cols])

        low, high = HALVES
        for t in range(TILES):
            if t > 0:
                nc.scalar.activation(h2[t][:], sums[t - 1][:], COPY)
            nc.vector.tensor_copy(pa2[t][:, :SPLIT], h2[t][:].indirect(n3_list[:, : SPLIT // 16]))
            if t > 0:
                fetch_gate(t - 1, high)
                gate(t - 1, high)
            fetch_gate(t, low)
            subtract(t, low)
            if t > 0:
                finish(t - 1, high)
            nc.scalar.activation(pa2[t][:, SPLIT:], h2[t][:].indirect(n3_list[:, SPLIT // 16 :]), COPY)
            gate(t, low)
            subtract(t, high)
            finish(t, low)
        for cols in QUARTERS[2:]:
            fetch_gate(TILES - 1, cols)
            gate(TILES - 1, cols)
        for cols in QUARTERS[2:]:
            finish(TILES - 1, cols)
